import numpy as np
import ml_dtypes


def mxq(x, axis, fmt="e4m3"):
    dtype, down = {"e4m3": (ml_dtypes.float8_e4m3fn, 7), "e5m2": (ml_dtypes.float8_e5m2, 14)}[fmt]
    v = np.moveaxis(np.asarray(x, np.float32).astype(ml_dtypes.bfloat16).astype(np.float64), axis, -1)
    blocks = v.reshape(v.shape[:-1] + (-1, 32))
    amax = np.abs(blocks).max(-1, keepdims=True)
    byte = np.maximum(np.where(amax > 0, np.frexp(amax)[1] - 1 + 127, 0) - down, 1)
    scale = np.exp2(byte - 127.0)
    codes = (blocks / scale).astype(np.float32).astype(dtype).astype(np.float64)
    return np.moveaxis((codes * scale).reshape(v.shape), -1, axis)


WIDE = False


def mx_kscale(k):
    if not WIDE:
        return np.ones(k)
    levels = np.array([10, -10, 5, -5, 0])
    if k % 512:
        return np.exp2(np.random.permutation(np.resize(levels, k // 32))).repeat(32)
    a = np.empty((k // 512, 16))
    for p in range(k // 512):
        a[p, :8] = np.random.permutation(np.resize(levels, 8))
        for g in range(8):
            far = levels[np.abs(levels - a[p, g]) >= 10]
            a[p, g + 8] = far[np.random.randint(len(far))]
    return np.exp2(a.ravel()).repeat(32)


def f64(x):
    return np.asarray(x).astype(np.float64)


def striped(idx):
    return np.tile(idx.reshape(-1, 16).T, (8, 1)).astype(np.uint16)


def unstriped(offs):
    return offs[:16].T.reshape(-1).astype(np.int64)

def planes(y):
    n, m = y.shape
    v = y.astype(np.float32).astype(ml_dtypes.bfloat16).astype(np.float64).reshape(n // 32, 32, m)
    top = np.abs(v).max(1)
    byte = np.clip(np.where(top > 0, np.frexp(top)[1] - 1 + 127 - 7, 1), 1, 254)
    codes = (v * np.exp2(127.0 - byte)[:, None, :]).reshape(n, m).astype(np.float32).astype(ml_dtypes.float8_e4m3fn).view(np.uint8)
    words = codes.reshape(n // 512, 128, 4, m).transpose(0, 1, 3, 2)
    return np.ascontiguousarray(words), np.ascontiguousarray(byte.astype(np.uint8).reshape(n // 512, 16, m))


K, T, S, V, H = 512, 1024, 512, 128, 512


def setup_inputs():
    n = np.random.standard_normal
    s = mx_kscale(K)[:, None]
    u = mx_kscale(H)
    return {
        "xT": (n((K, T)) * s).astype(np.float32),
        "w1": (n((K, H)) / np.sqrt(K) / s * u).astype(np.float32),
        "w2": (n((H, H)) / np.sqrt(2 * H) / u[:, None]).astype(np.float32),
        "w3": (n((H, H)) / np.sqrt(2 * H) / u[:, None]).astype(np.float32),
        "offs": striped(np.random.permutation(T)[:S]),
    }


def reference(xT, w1, w2, w3, offs):
    xq = mxq(f64(xT)[:, unstriped(offs)], 0, "e4m3")
    h = mxq(f64(w1), 0, "e4m3").T @ xq
    mean = (h[:, :V] + h[:, V:2 * V] + h[:, 2 * V:3 * V] + h[:, 3 * V:4 * V]) / 4
    dev = np.sqrt(((h[:, :V] - mean) ** 2 + (h[:, V:2 * V] - mean) ** 2 + (h[:, 2 * V:3 * V] - mean) ** 2 + (h[:, 3 * V:4 * V] - mean) ** 2) / 4)
    out_0 = mxq(f64(w2), 0, "e4m3").T @ mxq(mean, 0, "e4m3") + mxq(f64(w3), 0, "e4m3").T @ mxq(dev, 0, "e4m3")
    return (out_0,) + planes(out_0)

@@ -1,0 +1,179 @@
+from contextlib import ExitStack
+
+import concourse.mybir as mybir
+from concourse.masks import make_identity
+
+K, T, S, V, H = 512, 1024, 512, 128, 512
+D = S // V
+P = 128
+PACK = 4
+
+F32 = mybir.dt.float32
+BF16 = mybir.dt.bfloat16
+U32 = mybir.dt.uint32
+I32 = mybir.dt.int32
+U16 = mybir.dt.uint16
+U8 = mybir.dt.uint8
+FP8X4 = mybir.dt.float8_e4m3fn_x4
+ALU = mybir.AluOpType
+ACT = mybir.ActivationFunctionType
+
+FLOPS = 2 * K * H * S + 2 * 2 * H * H * V
+
+
+def tile_picked_statpool_none_lo_kernel(tc, xT, w1, w2, w3, offs, out_0, out_1, out_2):
+    nc = tc.nc
+    with ExitStack() as ctx:
+        keep = ctx.enter_context(tc.tile_pool(name="keep", bufs=1))
+        psum = ctx.enter_context(tc.psum_pool(name="psum", bufs=1))
+
+        def sbuf(name, shape, dtype, tag=""):
+            return keep.tile(shape, dtype, name=name, align_bytes=64, tag=tag or name)
+
+        def quantize(codes, scales, values):
+            nc.vector.quantize_mx(out=codes.bitcast(FP8X4), scales=scales, in_=values)
+
+        def product(out, a, b, start, stop):
+            nc.tensor.matmul_mx(out=out, lhsT=a[0].bitcast(FP8X4), lhsT_scale=a[1], rhs=b[0].bitcast(FP8X4), rhs_scale=b[1], start=start, stop=stop)
+
+        on_vector = nc.vector.tensor_copy
+        on_scalar = nc.scalar.copy
+
+        def on_gpsimd(out, in_):
+            nc.gpsimd.tensor_scalar(out=out, in0=in_, scalar1=1.0, scalar2=0.0, op0=ALU.mult, op1=ALU.add)
+
+        x_rows = xT.rearrange("(p j) n -> p j n", j=PACK)
+        offsets = keep.tile([P, S // 16], U16, name="offsets")
+        x_cuts = [[0,1024],[0,512,1024]]
+        x_raw = {}
+        for u in range(2):
+            for lo, hi in zip(x_cuts[u], x_cuts[u][1:]):
+                x_raw[u, lo, hi] = sbuf(f"x_raw{u}_{lo}", [P, 2, hi - lo], F32)
+                nc.sync.dma_start(out=x_raw[u, lo, hi][:], in_=x_rows[:, 2 * u : 2 * u + 2, lo:hi])
+                if u == 0 and lo == 0:
+                    nc.sync.dma_start(offsets[:], offs)
+        w_cuts = {"w1":[0,128],"w2":[0,128],"w3":[0,128]}
+        w_raw = {}
+        for name, w in (("w1", w1), ("w2", w2), ("w3", w3)):
+            rows = w.rearrange("(p j) n -> p j n", j=PACK)
+            for lo, hi in zip(w_cuts[name], w_cuts[name][1:]):
+                w_raw[name, lo, hi] = sbuf(f"{name}_raw{lo}", [P, PACK, PACK * (hi - lo)], F32)
+                nc.sync.dma_start(out=w_raw[name, lo, hi][:], in_=rows[:, :, PACK * lo : PACK * hi])
+
+        identity = sbuf("identity", [P, P], F32)
+        make_identity(nc, identity[:])
+        one_half = sbuf("one_half", [P, 1], F32)
+        root_half = sbuf("root_half", [P, 1], F32)
+        nc.gpsimd.memset(one_half[:], 0.5)
+        nc.scalar.activation(out=root_half[:], in_=one_half[:], func=ACT.Sqrt)
+
+        x_pairs = [sbuf(f"x_pairs{u}", [P, T, 2], BF16) for u in range(2)]
+        x_picked = sbuf("x_picked", [P, S, PACK], BF16)
+        x_codes = sbuf("x_codes", [P, S], U32)
+        x_scales = sbuf("x_scales", [P, S], U8)
+
+        def round_pairs(u, pieces):
+            for copy, a, b in pieces:
+                (lo, hi), = [(lo, hi) for (uu, lo, hi) in x_raw if uu == u and lo <= a and b <= hi]
+                copy(out=x_pairs[u][:, a:b, :], in_=x_raw[u, lo, hi][:, :, a - lo : b - lo].rearrange("p j n -> p n j"))
+
+        def gather(u, lo, hi):
+            window = x_pairs[u][:].rearrange("p n j -> p (n j)").bitcast(U32)
+            words = x_picked[:].rearrange("p s j -> p (s j)").bitcast(U32).rearrange("p (s u) -> p s u", u=2)
+            nc.vector.tensor_copy(words[:, lo:hi, u], window.indirect(offsets[:, lo // 16 : hi // 16]))
+
+        w_round = {}
+        w_codes = {n: sbuf(f"{n}_codes", [P, H], U32) for n in ("w1", "w2", "w3")}
+        w_scales = {n: sbuf(f"{n}_scales", [P, H], U8) for n in ("w1", "w2", "w3")}
+
+        def round_weights(name, pieces, tag):
+            w_round[name] = sbuf(f"{name}_round", [P, PACK, P, PACK], BF16, tag)
+            for copy, a, b in pieces:
+                (lo, hi), = [(lo, hi) for (n, lo, hi) in w_raw if n == name and lo <= a and b <= hi]
+                src = w_raw[name, lo, hi][:].rearrange("p j (m t) -> p m t j", t=PACK)[:, a - lo : b - lo]
+                copy(out=w_round[name][:].rearrange("p t m j -> p m t j")[:, a:b], in_=src)
+
+        def quantize_weights(name, t0, t1):
+            cols = slice(t0 * P, t1 * P)
+            quantize(w_codes[name][:, cols], w_scales[name][:, cols], w_round[name][:, t0:t1].rearrange("p t m j -> p (t m j)"))
+
+        def weights(name, t):
+            cols = slice(t * P, (t + 1) * P)
+            return w_codes[name][:, cols], w_scales[name][:, cols]
+
+        round_pairs(0, [(on_vector, 0, 704), (on_scalar, 704, 1024)])
+        gather(0, 0, S)
+        round_pairs(1, [(on_scalar, 0, 512), (on_vector, 512, 1024)])
+        gather(1, 0, S // 2)
+        gather(1, S // 2, S)
+        for c in range(2):
+            cols = slice(c * S // 2, (c + 1) * S // 2)
+            quantize(x_codes[:, cols], x_scales[:, cols], x_picked[:, cols].rearrange("p s j -> p (s j)"))
+
+        round_weights("w1", [(on_vector, 0, 80), (on_scalar, 80, 128)], "round_a")
+        quantize_weights("w1", 0, 1)
+        quantize_weights("w1", 1, 2)
+        quantize_weights("w1", 2, 4)
+
+        h = [psum.tile([P, D, P], F32, name=f"h{t}", tag=f"bank{t}") for t in range(PACK)]
+        for t in range(PACK):
+            for d in range(D):
+                cols = slice(d * V, (d + 1) * V)
+                product(h[t][:, d, :], (x_codes[:, cols], x_scales[:, cols]), weights("w1", t), True, True)
+
+        sum_bank = psum.tile([P, PACK, V], F32, name="sum_bank")
+        var_bank = psum.tile([P, PACK, V], F32, name="var_bank")
+        for t in range(PACK):
+            upper = sbuf(f"upper{t}", [P, 2, P], F32)
+            diff = sbuf(f"diff{t}", [P, 2, P], F32)
+            sums = sbuf(f"sums{t}", [P, 2, P], F32)
+            cross = sbuf(f"cross{t}", [P, P], F32)
+            squares = sbuf(f"squares{t}", [P, 3, P], F32)
+            nc.scalar.copy(out=upper[:], in_=h[t][:, 2:4, :])
+            nc.vector.tensor_tensor(out=sums[:], in0=h[t][:, 0:2, :], in1=upper[:], op=ALU.add)
+            nc.vector.tensor_tensor(out=diff[:], in0=h[t][:, 0:2, :], in1=upper[:], op=ALU.subtract)
+            nc.scalar.activation(out=squares[:, 0:2, :], in_=diff[:], func=ACT.Square)
+            engine = nc.gpsimd if t < 0 else nc.vector
+            engine.tensor_tensor(out=cross[:], in0=sums[:, 0, :], in1=sums[:, 1, :], op=ALU.subtract)
+            nc.scalar.activation(out=squares[:, 2, :], in_=cross[:], func=ACT.Square, scale=root_half[:])
+            for e in range(2):
+                nc.tensor.matmul(out=sum_bank[:, t, :], lhsT=sums[:, e, :], rhs=identity[:], start=(e == 0), stop=(e == 1), is_transpose=True)
+            for e in range(3):
+                nc.tensor.matmul(out=var_bank[:, t, :], lhsT=squares[:, e, :], rhs=identity[:], start=(e == 0), stop=(e == 2), is_transpose=True)
+
+        mean = sbuf("mean", [P, V, PACK], BF16)
+        dev = sbuf("dev", [P, V, PACK], BF16)
+        nc.vector.tensor_scalar(out=mean[:], in0=sum_bank[:].rearrange("p t v -> p v t"), scalar1=1.0 / D, scalar2=None, op0=ALU.mult)
+        nc.scalar.activation(out=dev[:], in_=var_bank[:].rearrange("p t v -> p v t"), func=ACT.Sqrt, scale=0.125)
+        stat = {}
+        for name, values in (("w3", dev), ("w2", mean)):
+            codes = sbuf(f"stat_codes_{name}", [P, V], U32)
+            scales = sbuf(f"stat_scales_{name}", [P, V], U8)
+            quantize(codes[:], scales[:], values[:].rearrange("p v t -> p (v t)"))
+            stat[name] = (codes[:], scales[:])
+
+        round_weights("w2", [(on_scalar, 0, 24), (on_scalar, 24, 48), (on_scalar, 48, 72), (on_scalar, 72, 96), (on_vector, 96, 128)], "round_b")
+        quantize_weights("w2", 0, 4)
+        round_weights("w3", [(on_scalar, 0, 32), (on_scalar, 32, 64), (on_vector, 64, 96), (on_vector, 96, 128)], "round_c")
+        quantize_weights("w3", 0, 2)
+        quantize_weights("w3", 2, 4)
+
+        tags = ["bank_y0", "bank_y1", "bank0", "bank1"]
+        y_banks = [psum.tile([P, V], F32, name=f"y{t}", tag=tags[t]) for t in range(PACK)]
+        for name in ("w2", "w3"):
+            for t in range(PACK):
+                product(y_banks[t][:], weights(name, t), stat[name], name == "w2", name == "w3")
+        y = sbuf("y", [P, PACK, V], F32)
+        for t in range(PACK):
+            copy = on_scalar if t % 2 == 0 else on_vector
+            copy(out=y[:, t, :], in_=y_banks[t][:])
+        nc.sync.dma_start(out=out_0.rearrange("(p t) v -> p t v", t=PACK), in_=y[:])
+        y_round = sbuf("y_round", [P, V, PACK], BF16)
+        y_codes = sbuf("y_codes", [P, V], U32)
+        y_scales = sbuf("y_scales", [P, V], U8)
+        nc.vector.tensor_copy(out=y_round[:], in_=y[:].rearrange("p t v -> p v t"))
+        quantize(y_codes[:], y_scales[:], y_round[:].rearrange("p v t -> p (v t)"))
+        nc.sync.dma_start(out=out_1[0].rearrange("p c r -> p (c r)").bitcast(I32), in_=y_codes[:].bitcast(I32))
+        for q in range(4):
+            queue = nc.scalar if q % 2 == 0 else nc.sync
+            queue.dma_start(out=out_2[0, 4 * q : 4 * q + 4, :].bitcast(I32), in_=y_scales[32 * q : 32 * q + 4, :].bitcast(I32))

@@ -7,6 +7,9 @@ K, T, S, V, H = 512, 1024, 512, 128, 512
 D = S // V
 P = 128
 PACK = 4
+OPERAND = P * PACK
+LIST_ROWS = 16
+QUADRANT = 32
 
 F32 = mybir.dt.float32
 BF16 = mybir.dt.bfloat16
@@ -20,45 +23,61 @@ ACT = mybir.ActivationFunctionType
 
 FLOPS = 2 * K * H * S + 2 * 2 * H * H * V
 
+X_LOADS = ((0, 0, 640), (0, 640, T), (1, 0, 640), (1, 640, T))
+X_SHARES = (
+    ((0, "vector", 0, 640), (1, "vector", 640, 896), (1, "scalar", 896, T)),
+    ((2, "scalar", 0, 384), (2, "vector", 384, 640), (3, "vector", 640, 896), (3, "scalar", 896, T)),
+)
+RUNS = ((0, 2), (2, 3), (3, 4))
+ROW = (("x", 0), ("x", 1), ("x", 2), ("w1", 0), ("w1", 1), ("x", 3))
+ROW_CALLS = ((0, 4), (4, 6))
+W1_LATE_SHARES = (("vector", 64, P), ("scalar", 0, 64))
+W_SHARES = {
+    "w2": (("scalar", 0, 16), ("scalar", 16, 32), ("scalar", 32, 48), ("scalar", 48, 64), ("vector", 64, 96), ("vector", 96, P)),
+    "w3": (("vector", 0, 64), ("vector", 64, P)),
+}
+
 
 def tile_picked_statpool_none_lo_kernel(tc, xT, w1, w2, w3, offs, out_0, out_1, out_2):
     nc = tc.nc
+    copy_on = {"vector": nc.vector.tensor_copy, "scalar": nc.scalar.copy}
     with ExitStack() as ctx:
         keep = ctx.enter_context(tc.tile_pool(name="keep", bufs=1))
         psum = ctx.enter_context(tc.psum_pool(name="psum", bufs=1))
 
-        def sbuf(name, shape, dtype, tag=""):
-            return keep.tile(shape, dtype, name=name, align_bytes=64, tag=tag or name)
+        def sbuf(name, shape, dtype):
+            return keep.tile(shape, dtype, name=name, align_bytes=64, tag=name)
 
         def quantize(codes, scales, values):
             nc.vector.quantize_mx(out=codes.bitcast(FP8X4), scales=scales, in_=values)
 
-        def product(out, a, b, start, stop):
-            nc.tensor.matmul_mx(out=out, lhsT=a[0].bitcast(FP8X4), lhsT_scale=a[1], rhs=b[0].bitcast(FP8X4), rhs_scale=b[1], start=start, stop=stop)
+        def product(out, stationary, moving, start, stop):
+            nc.tensor.matmul_mx(
+                out=out,
+                lhsT=stationary[0].bitcast(FP8X4),
+                lhsT_scale=stationary[1],
+                rhs=moving[0].bitcast(FP8X4),
+                rhs_scale=moving[1],
+                start=start,
+                stop=stop,
+            )
 
-        on_vector = nc.vector.tensor_copy
-        on_scalar = nc.scalar.copy
+        def add_transposed(out, terms, count):
+            for e in range(count):
+                nc.tensor.matmul(out=out, lhsT=terms[:, e, :], rhs=identity[:], start=(e == 0), stop=(e == count - 1), is_transpose=True)
 
-        def on_gpsimd(out, in_):
-            nc.gpsimd.tensor_scalar(out=out, in0=in_, scalar1=1.0, scalar2=0.0, op0=ALU.mult, op1=ALU.add)
-
-        x_rows = xT.rearrange("(p j) n -> p j n", j=PACK)
-        offsets = keep.tile([P, S // 16], U16, name="offsets")
-        x_cuts = [[0,1024],[0,512,1024]]
-        x_raw = {}
-        for u in range(2):
-            for lo, hi in zip(x_cuts[u], x_cuts[u][1:]):
-                x_raw[u, lo, hi] = sbuf(f"x_raw{u}_{lo}", [P, 2, hi - lo], F32)
-                nc.sync.dma_start(out=x_raw[u, lo, hi][:], in_=x_rows[:, 2 * u : 2 * u + 2, lo:hi])
-                if u == 0 and lo == 0:
-                    nc.sync.dma_start(offsets[:], offs)
-        w_cuts = {"w1":[0,128],"w2":[0,128],"w3":[0,128]}
+        x_rows = xT.rearrange("(p t) n -> p t n", t=PACK)
+        offsets = keep.tile([P, S // LIST_ROWS], U16, name="offsets")
+        x_raw = []
+        for pair, lo, hi in X_LOADS:
+            x_raw.append(sbuf(f"x_raw{pair}_{lo}", [P, 2, hi - lo], F32))
+            nc.sync.dma_start(out=x_raw[-1][:], in_=x_rows[:, 2 * pair : 2 * pair + 2, lo:hi])
+            if pair == 0 and lo == 0:
+                nc.sync.dma_start(offsets[:], offs)
         w_raw = {}
         for name, w in (("w1", w1), ("w2", w2), ("w3", w3)):
-            rows = w.rearrange("(p j) n -> p j n", j=PACK)
-            for lo, hi in zip(w_cuts[name], w_cuts[name][1:]):
-                w_raw[name, lo, hi] = sbuf(f"{name}_raw{lo}", [P, PACK, PACK * (hi - lo)], F32)
-                nc.sync.dma_start(out=w_raw[name, lo, hi][:], in_=rows[:, :, PACK * lo : PACK * hi])
+            w_raw[name] = sbuf(f"{name}_raw0", [P, PACK, H], F32)
+            nc.sync.dma_start(out=w_raw[name][:], in_=w.rearrange("(p j) n -> p j n", j=PACK))
 
         identity = sbuf("identity", [P, P], F32)
         make_identity(nc, identity[:])
@@ -67,113 +86,132 @@ def tile_picked_statpool_none_lo_kernel(tc, xT, w1, w2, w3, offs, out_0, out_1, 
         nc.gpsimd.memset(one_half[:], 0.5)
         nc.scalar.activation(out=root_half[:], in_=one_half[:], func=ACT.Sqrt)
 
-        x_pairs = [sbuf(f"x_pairs{u}", [P, T, 2], BF16) for u in range(2)]
-        x_picked = sbuf("x_picked", [P, S, PACK], BF16)
-        x_codes = sbuf("x_codes", [P, S], U32)
-        x_scales = sbuf("x_scales", [P, S], U8)
+        x_pairs = [sbuf(f"x_pairs{pair}", [P, T, 2], BF16) for pair in range(2)]
+        row_values = sbuf("first_round", [P, len(ROW) * OPERAND], BF16)
+        row_codes = sbuf("first_codes", [P, len(ROW) * P], U32)
+        row_scales = sbuf("first_scales", [P, len(ROW) * P], U8)
+        gathered = [sbuf(f"gathered{d0}", [P, 2, (d1 - d0) * V], U32) for d0, d1 in RUNS]
+        w_codes = {name: sbuf(f"{name}_codes", [P, H], U32) for name in w_raw}
+        w_scales = {name: sbuf(f"{name}_scales", [P, H], U8) for name in w_raw}
 
-        def round_pairs(u, pieces):
-            for copy, a, b in pieces:
-                (lo, hi), = [(lo, hi) for (uu, lo, hi) in x_raw if uu == u and lo <= a and b <= hi]
-                copy(out=x_pairs[u][:, a:b, :], in_=x_raw[u, lo, hi][:, :, a - lo : b - lo].rearrange("p j n -> p n j"))
-
-        def gather(u, lo, hi):
-            window = x_pairs[u][:].rearrange("p n j -> p (n j)").bitcast(U32)
-            words = x_picked[:].rearrange("p s j -> p (s j)").bitcast(U32).rearrange("p (s u) -> p s u", u=2)
-            nc.vector.tensor_copy(words[:, lo:hi, u], window.indirect(offsets[:, lo // 16 : hi // 16]))
-
-        w_round = {}
-        w_codes = {n: sbuf(f"{n}_codes", [P, H], U32) for n in ("w1", "w2", "w3")}
-        w_scales = {n: sbuf(f"{n}_scales", [P, H], U8) for n in ("w1", "w2", "w3")}
-
-        def round_weights(name, pieces, tag):
-            w_round[name] = sbuf(f"{name}_round", [P, PACK, P, PACK], BF16, tag)
-            for copy, a, b in pieces:
-                (lo, hi), = [(lo, hi) for (n, lo, hi) in w_raw if n == name and lo <= a and b <= hi]
-                src = w_raw[name, lo, hi][:].rearrange("p j (m t) -> p m t j", t=PACK)[:, a - lo : b - lo]
-                copy(out=w_round[name][:].rearrange("p t m j -> p m t j")[:, a:b], in_=src)
-
-        def quantize_weights(name, t0, t1):
-            cols = slice(t0 * P, t1 * P)
-            quantize(w_codes[name][:, cols], w_scales[name][:, cols], w_round[name][:, t0:t1].rearrange("p t m j -> p (t m j)"))
-
-        def weights(name, t):
-            cols = slice(t * P, (t + 1) * P)
+        def operand(name, n):
+            if (name, n) in ROW:
+                place = ROW.index((name, n))
+                cols = slice(place * P, (place + 1) * P)
+                return row_codes[:, cols], row_scales[:, cols]
+            cols = slice(n * P, (n + 1) * P)
             return w_codes[name][:, cols], w_scales[name][:, cols]
 
-        round_pairs(0, [(on_vector, 0, 704), (on_scalar, 704, 1024)])
-        gather(0, 0, S)
-        round_pairs(1, [(on_scalar, 0, 512), (on_vector, 512, 1024)])
-        gather(1, 0, S // 2)
-        gather(1, S // 2, S)
-        for c in range(2):
-            cols = slice(c * S // 2, (c + 1) * S // 2)
-            quantize(x_codes[:, cols], x_scales[:, cols], x_picked[:, cols].rearrange("p s j -> p (s j)"))
+        def round_pair(pair):
+            for load, engine, a, b in X_SHARES[pair]:
+                lo = X_LOADS[load][1]
+                copy_on[engine](out=x_pairs[pair][:, a:b, :], in_=x_raw[load][:, :, a - lo : b - lo].rearrange("p t n -> p n t"))
 
-        round_weights("w1", [(on_vector, 0, 80), (on_scalar, 80, 128)], "round_a")
-        quantize_weights("w1", 0, 1)
-        quantize_weights("w1", 1, 2)
-        quantize_weights("w1", 2, 4)
+        def gather(pair, run):
+            d0, d1 = RUNS[run]
+            window = x_pairs[pair][:].rearrange("p n t -> p (n t)").bitcast(U32)
+            entries = offsets[:, d0 * V // LIST_ROWS : d1 * V // LIST_ROWS]
+            nc.vector.tensor_copy(gathered[run][:, pair, :], window.indirect(entries))
 
-        h = [psum.tile([P, D, P], F32, name=f"h{t}", tag=f"bank{t}") for t in range(PACK)]
+        def join_pairs(run):
+            d0, d1 = RUNS[run]
+            start = ROW.index(("x", d0)) * OPERAND
+            words = row_values[:, start : start + (d1 - d0) * OPERAND].bitcast(U32).rearrange("p (s u) -> p s u", u=2)
+            nc.scalar.copy(out=words, in_=gathered[run][:].rearrange("p u s -> p s u"))
+
+        def round_w1(target, half, engine, a, b):
+            source = w_raw["w1"][:].rearrange("p j (m e t) -> p e j m t", e=2, t=2)[:, half, :, a:b]
+            copy_on[engine](out=target.rearrange("p t m j -> p m j t")[:, a:b], in_=source.rearrange("p j m t -> p m j t"))
+
+        def quantize_two_tiles(name, t0, values):
+            cols = slice(t0 * P, (t0 + 2) * P)
+            quantize(w_codes[name][:, cols], w_scales[name][:, cols], values.rearrange("p t m j -> p (t m j)"))
+
+        round_pair(0)
+        for run in range(len(RUNS)):
+            gather(0, run)
+        round_pair(1)
+        for run in range(len(RUNS)):
+            gather(1, run)
+            join_pairs(run)
+        w1_start = ROW.index(("w1", 0)) * OPERAND
+        w1_early = row_values[:, w1_start : w1_start + 2 * OPERAND].rearrange("p (t m j) -> p t m j", t=2, j=PACK)
+        round_w1(w1_early, 0, "vector", 0, P)
+        w1_late = sbuf("w1_round1", [P, 2, P, PACK], BF16)
+        for engine, a, b in W1_LATE_SHARES:
+            round_w1(w1_late[:], 1, engine, a, b)
+        for a, b in ROW_CALLS:
+            quantize(row_codes[:, a * P : b * P], row_scales[:, a * P : b * P], row_values[:, a * OPERAND : b * OPERAND])
+        quantize_two_tiles("w1", 2, w1_late[:])
+
+        h_banks = [psum.tile([P, D, P], F32, name=f"h{t}", tag=f"bank{t}") for t in range(PACK)]
+        early_bank = psum.tile([P, 2, P], F32, name="early", tag="bank_y0")
+        h01 = [early_bank[:]] + [h_banks[t][:, 0:2, :] for t in range(1, PACK)]
+        h23 = [h_banks[t][:, 2:4, :] for t in range(PACK)]
         for t in range(PACK):
             for d in range(D):
-                cols = slice(d * V, (d + 1) * V)
-                product(h[t][:, d, :], (x_codes[:, cols], x_scales[:, cols]), weights("w1", t), True, True)
+                target = h01[t][:, d, :] if d < 2 else h23[t][:, d - 2, :]
+                product(target, operand("x", d), operand("w1", t), True, True)
 
         sum_bank = psum.tile([P, PACK, V], F32, name="sum_bank")
         var_bank = psum.tile([P, PACK, V], F32, name="var_bank")
         for t in range(PACK):
-            upper = sbuf(f"upper{t}", [P, 2, P], F32)
+            h01_copy = sbuf(f"upper{t}", [P, 2, P], F32)
             diff = sbuf(f"diff{t}", [P, 2, P], F32)
             sums = sbuf(f"sums{t}", [P, 2, P], F32)
             cross = sbuf(f"cross{t}", [P, P], F32)
             squares = sbuf(f"squares{t}", [P, 3, P], F32)
-            nc.scalar.copy(out=upper[:], in_=h[t][:, 2:4, :])
-            nc.vector.tensor_tensor(out=sums[:], in0=h[t][:, 0:2, :], in1=upper[:], op=ALU.add)
-            nc.vector.tensor_tensor(out=diff[:], in0=h[t][:, 0:2, :], in1=upper[:], op=ALU.subtract)
+            nc.scalar.copy(out=h01_copy[:], in_=h01[t])
+            nc.vector.tensor_tensor(out=sums[:], in0=h23[t], in1=h01_copy[:], op=ALU.add)
+            nc.vector.tensor_tensor(out=diff[:], in0=h23[t], in1=h01_copy[:], op=ALU.subtract)
             nc.scalar.activation(out=squares[:, 0:2, :], in_=diff[:], func=ACT.Square)
-            engine = nc.gpsimd if t < 0 else nc.vector
+            engine = nc.gpsimd if t < PACK - 1 else nc.vector
             engine.tensor_tensor(out=cross[:], in0=sums[:, 0, :], in1=sums[:, 1, :], op=ALU.subtract)
             nc.scalar.activation(out=squares[:, 2, :], in_=cross[:], func=ACT.Square, scale=root_half[:])
-            for e in range(2):
-                nc.tensor.matmul(out=sum_bank[:, t, :], lhsT=sums[:, e, :], rhs=identity[:], start=(e == 0), stop=(e == 1), is_transpose=True)
-            for e in range(3):
-                nc.tensor.matmul(out=var_bank[:, t, :], lhsT=squares[:, e, :], rhs=identity[:], start=(e == 0), stop=(e == 2), is_transpose=True)
+            add_transposed(sum_bank[:, t, :], sums, 2)
+            add_transposed(var_bank[:, t, :], squares, 3)
 
         mean = sbuf("mean", [P, V, PACK], BF16)
         dev = sbuf("dev", [P, V, PACK], BF16)
-        nc.vector.tensor_scalar(out=mean[:], in0=sum_bank[:].rearrange("p t v -> p v t"), scalar1=1.0 / D, scalar2=None, op0=ALU.mult)
+        nc.scalar.activation(out=mean[:], in_=sum_bank[:].rearrange("p t v -> p v t"), func=ACT.Copy, scale=1.0 / D)
         nc.scalar.activation(out=dev[:], in_=var_bank[:].rearrange("p t v -> p v t"), func=ACT.Sqrt, scale=0.125)
-        stat = {}
+        partner = {}
         for name, values in (("w3", dev), ("w2", mean)):
             codes = sbuf(f"stat_codes_{name}", [P, V], U32)
             scales = sbuf(f"stat_scales_{name}", [P, V], U8)
             quantize(codes[:], scales[:], values[:].rearrange("p v t -> p (v t)"))
-            stat[name] = (codes[:], scales[:])
+            partner[name] = (codes[:], scales[:])
 
-        round_weights("w2", [(on_scalar, 0, 24), (on_scalar, 24, 48), (on_scalar, 48, 72), (on_scalar, 72, 96), (on_vector, 96, 128)], "round_b")
-        quantize_weights("w2", 0, 4)
-        round_weights("w3", [(on_scalar, 0, 32), (on_scalar, 32, 64), (on_vector, 64, 96), (on_vector, 96, 128)], "round_c")
-        quantize_weights("w3", 0, 2)
-        quantize_weights("w3", 2, 4)
+        for name in ("w2", "w3"):
+            rounded = sbuf(f"{name}_round", [P, PACK, P, PACK], BF16)
+            source = w_raw[name][:].rearrange("p j (m t) -> p m j t", t=PACK)
+            for engine, a, b in W_SHARES[name]:
+                copy_on[engine](out=rounded[:].rearrange("p t m j -> p m j t")[:, a:b], in_=source[:, a:b])
+            for t0 in (0, 2):
+                quantize_two_tiles(name, t0, rounded[:, t0 : t0 + 2])
 
-        tags = ["bank_y0", "bank_y1", "bank0", "bank1"]
-        y_banks = [psum.tile([P, V], F32, name=f"y{t}", tag=tags[t]) for t in range(PACK)]
+        y_tags = ("bank_y0", "bank_y1", "bank0", "bank1")
+        y_banks = [psum.tile([P, V], F32, name=f"y{t}", tag=y_tags[t]) for t in range(PACK)]
         for name in ("w2", "w3"):
             for t in range(PACK):
-                product(y_banks[t][:], weights(name, t), stat[name], name == "w2", name == "w3")
+                product(y_banks[t][:], operand(name, t), partner[name], name == "w2", name == "w3")
         y = sbuf("y", [P, PACK, V], F32)
         for t in range(PACK):
-            copy = on_scalar if t % 2 == 0 else on_vector
-            copy(out=y[:, t, :], in_=y_banks[t][:])
+            copy_on["scalar" if t % 2 == 0 else "vector"](out=y[:, t, :], in_=y_banks[t][:])
         nc.sync.dma_start(out=out_0.rearrange("(p t) v -> p t v", t=PACK), in_=y[:])
+
         y_round = sbuf("y_round", [P, V, PACK], BF16)
         y_codes = sbuf("y_codes", [P, V], U32)
         y_scales = sbuf("y_scales", [P, V], U8)
-        nc.vector.tensor_copy(out=y_round[:], in_=y[:].rearrange("p t v -> p v t"))
+        nc.vector.tensor_copy(
+            out=y_round[:].rearrange("p (c i) t -> p c t i", i=4),
+            in_=y[:].rearrange("p t (c i) -> p c t i", i=4),
+        )
         quantize(y_codes[:], y_scales[:], y_round[:].rearrange("p v t -> p (v t)"))
         nc.sync.dma_start(out=out_1[0].rearrange("p c r -> p (c r)").bitcast(I32), in_=y_codes[:].bitcast(I32))
-        for q in range(4):
-            queue = nc.scalar if q % 2 == 0 else nc.sync
-            queue.dma_start(out=out_2[0, 4 * q : 4 * q + 4, :].bitcast(I32), in_=y_scales[32 * q : 32 * q + 4, :].bitcast(I32))
+        for g in range(P // QUADRANT):
+            queue = nc.scalar if g % 2 == 0 else nc.sync
+            queue.dma_start(
+                out=out_2[0, 4 * g : 4 * g + 4, :].bitcast(I32),
+                in_=y_scales[QUADRANT * g : QUADRANT * g + 4, :].bitcast(I32),
+            )

from contextlib import ExitStack

import concourse.mybir as mybir
from concourse.masks import make_identity

K, T, S, V, H = 512, 1024, 512, 128, 512
D = S // V
P = 128
PACK = 4
OPERAND = P * PACK
LIST_ROWS = 16
QUADRANT = 32

F32 = mybir.dt.float32
BF16 = mybir.dt.bfloat16
U32 = mybir.dt.uint32
I32 = mybir.dt.int32
U16 = mybir.dt.uint16
U8 = mybir.dt.uint8
FP8X4 = mybir.dt.float8_e4m3fn_x4
ALU = mybir.AluOpType
ACT = mybir.ActivationFunctionType

FLOPS = 2 * K * H * S + 2 * 2 * H * H * V

X_LOADS = ((0, 0, 640), (0, 640, T), (1, 0, 640), (1, 640, T))
X_SHARES = (
    ((0, "vector", 0, 640), (1, "vector", 640, 896), (1, "scalar", 896, T)),
    ((2, "scalar", 0, 384), (2, "vector", 384, 640), (3, "vector", 640, 896), (3, "scalar", 896, T)),
)
RUNS = ((0, 2), (2, 3), (3, 4))
ROW = (("x", 0), ("x", 1), ("x", 2), ("w1", 0), ("w1", 1), ("x", 3))
ROW_CALLS = ((0, 4), (4, 6))
W1_LATE_SHARES = (("vector", 64, P), ("scalar", 0, 64))
W_SHARES = {
    "w2": (("scalar", 0, 16), ("scalar", 16, 32), ("scalar", 32, 48), ("scalar", 48, 64), ("vector", 64, 96), ("vector", 96, P)),
    "w3": (("vector", 0, 64), ("vector", 64, P)),
}


def tile_picked_statpool_none_lo_kernel(tc, xT, w1, w2, w3, offs, out_0, out_1, out_2):
    nc = tc.nc
    copy_on = {"vector": nc.vector.tensor_copy, "scalar": nc.scalar.copy}
    with ExitStack() as ctx:
        keep = ctx.enter_context(tc.tile_pool(name="keep", bufs=1))
        psum = ctx.enter_context(tc.psum_pool(name="psum", bufs=1))

        def sbuf(name, shape, dtype):
            return keep.tile(shape, dtype, name=name, align_bytes=64, tag=name)

        def quantize(codes, scales, values):
            nc.vector.quantize_mx(out=codes.bitcast(FP8X4), scales=scales, in_=values)

        def product(out, stationary, moving, start, stop):
            nc.tensor.matmul_mx(
                out=out,
                lhsT=stationary[0].bitcast(FP8X4),
                lhsT_scale=stationary[1],
                rhs=moving[0].bitcast(FP8X4),
                rhs_scale=moving[1],
                start=start,
                stop=stop,
            )

        def add_transposed(out, terms, count):
            for e in range(count):
                nc.tensor.matmul(out=out, lhsT=terms[:, e, :], rhs=identity[:], start=(e == 0), stop=(e == count - 1), is_transpose=True)

        x_rows = xT.rearrange("(p t) n -> p t n", t=PACK)
        offsets = keep.tile([P, S // LIST_ROWS], U16, name="offsets")
        x_raw = []
        for pair, lo, hi in X_LOADS:
            x_raw.append(sbuf(f"x_raw{pair}_{lo}", [P, 2, hi - lo], F32))
            nc.sync.dma_start(out=x_raw[-1][:], in_=x_rows[:, 2 * pair : 2 * pair + 2, lo:hi])
            if pair == 0 and lo == 0:
                nc.sync.dma_start(offsets[:], offs)
        w_raw = {}
        for name, w in (("w1", w1), ("w2", w2), ("w3", w3)):
            w_raw[name] = sbuf(f"{name}_raw0", [P, PACK, H], F32)
            nc.sync.dma_start(out=w_raw[name][:], in_=w.rearrange("(p j) n -> p j n", j=PACK))

        identity = sbuf("identity", [P, P], F32)
        make_identity(nc, identity[:])
        one_half = sbuf("one_half", [P, 1], F32)
        root_half = sbuf("root_half", [P, 1], F32)
        nc.gpsimd.memset(one_half[:], 0.5)
        nc.scalar.activation(out=root_half[:], in_=one_half[:], func=ACT.Sqrt)

        x_pairs = [sbuf(f"x_pairs{pair}", [P, T, 2], BF16) for pair in range(2)]
        row_values = sbuf("first_round", [P, len(ROW) * OPERAND], BF16)
        row_codes = sbuf("first_codes", [P, len(ROW) * P], U32)
        row_scales = sbuf("first_scales", [P, len(ROW) * P], U8)
        gathered = [sbuf(f"gathered{d0}", [P, 2, (d1 - d0) * V], U32) for d0, d1 in RUNS]
        w_codes = {name: sbuf(f"{name}_codes", [P, H], U32) for name in w_raw}
        w_scales = {name: sbuf(f"{name}_scales", [P, H], U8) for name in w_raw}

        def operand(name, n):
            if (name, n) in ROW:
                place = ROW.index((name, n))
                cols = slice(place * P, (place + 1) * P)
                return row_codes[:, cols], row_scales[:, cols]
            cols = slice(n * P, (n + 1) * P)
            return w_codes[name][:, cols], w_scales[name][:, cols]

        def round_pair(pair):
            for load, engine, a, b in X_SHARES[pair]:
                lo = X_LOADS[load][1]
                copy_on[engine](out=x_pairs[pair][:, a:b, :], in_=x_raw[load][:, :, a - lo : b - lo].rearrange("p t n -> p n t"))

        def gather(pair, run):
            d0, d1 = RUNS[run]
            window = x_pairs[pair][:].rearrange("p n t -> p (n t)").bitcast(U32)
            entries = offsets[:, d0 * V // LIST_ROWS : d1 * V // LIST_ROWS]
            nc.vector.tensor_copy(gathered[run][:, pair, :], window.indirect(entries))

        def join_pairs(run):
            d0, d1 = RUNS[run]
            start = ROW.index(("x", d0)) * OPERAND
            words = row_values[:, start : start + (d1 - d0) * OPERAND].bitcast(U32).rearrange("p (s u) -> p s u", u=2)
            nc.scalar.copy(out=words, in_=gathered[run][:].rearrange("p u s -> p s u"))

        def round_w1(target, half, engine, a, b):
            source = w_raw["w1"][:].rearrange("p j (m e t) -> p e j m t", e=2, t=2)[:, half, :, a:b]
            copy_on[engine](out=target.rearrange("p t m j -> p m j t")[:, a:b], in_=source.rearrange("p j m t -> p m j t"))

        def quantize_two_tiles(name, t0, values):
            cols = slice(t0 * P, (t0 + 2) * P)
            quantize(w_codes[name][:, cols], w_scales[name][:, cols], values.rearrange("p t m j -> p (t m j)"))

        round_pair(0)
        for run in range(len(RUNS)):
            gather(0, run)
        round_pair(1)
        for run in range(len(RUNS)):
            gather(1, run)
            join_pairs(run)
        w1_start = ROW.index(("w1", 0)) * OPERAND
        w1_early = row_values[:, w1_start : w1_start + 2 * OPERAND].rearrange("p (t m j) -> p t m j", t=2, j=PACK)
        round_w1(w1_early, 0, "vector", 0, P)
        w1_late = sbuf("w1_round1", [P, 2, P, PACK], BF16)
        for engine, a, b in W1_LATE_SHARES:
            round_w1(w1_late[:], 1, engine, a, b)
        for a, b in ROW_CALLS:
            quantize(row_codes[:, a * P : b * P], row_scales[:, a * P : b * P], row_values[:, a * OPERAND : b * OPERAND])
        quantize_two_tiles("w1", 2, w1_late[:])

        h_banks = [psum.tile([P, D, P], F32, name=f"h{t}", tag=f"bank{t}") for t in range(PACK)]
        early_bank = psum.tile([P, 2, P], F32, name="early", tag="bank_y0")
        h01 = [early_bank[:]] + [h_banks[t][:, 0:2, :] for t in range(1, PACK)]
        h23 = [h_banks[t][:, 2:4, :] for t in range(PACK)]
        for t in range(PACK):
            for d in range(D):
                target = h01[t][:, d, :] if d < 2 else h23[t][:, d - 2, :]
                product(target, operand("x", d), operand("w1", t), True, True)

        sum_bank = psum.tile([P, PACK, V], F32, name="sum_bank")
        var_bank = psum.tile([P, PACK, V], F32, name="var_bank")
        for t in range(PACK):
            h01_copy = sbuf(f"upper{t}", [P, 2, P], F32)
            diff = sbuf(f"diff{t}", [P, 2, P], F32)
            sums = sbuf(f"sums{t}", [P, 2, P], F32)
            cross = sbuf(f"cross{t}", [P, P], F32)
            squares = sbuf(f"squares{t}", [P, 3, P], F32)
            nc.scalar.copy(out=h01_copy[:], in_=h01[t])
            nc.vector.tensor_tensor(out=sums[:], in0=h23[t], in1=h01_copy[:], op=ALU.add)
            nc.vector.tensor_tensor(out=diff[:], in0=h23[t], in1=h01_copy[:], op=ALU.subtract)
            nc.scalar.activation(out=squares[:, 0:2, :], in_=diff[:], func=ACT.Square)
            engine = nc.gpsimd if t < PACK - 1 else nc.vector
            engine.tensor_tensor(out=cross[:], in0=sums[:, 0, :], in1=sums[:, 1, :], op=ALU.subtract)
            nc.scalar.activation(out=squares[:, 2, :], in_=cross[:], func=ACT.Square, scale=root_half[:])
            add_transposed(sum_bank[:, t, :], sums, 2)
            add_transposed(var_bank[:, t, :], squares, 3)

        mean = sbuf("mean", [P, V, PACK], BF16)
        dev = sbuf("dev", [P, V, PACK], BF16)
        nc.scalar.activation(out=mean[:], in_=sum_bank[:].rearrange("p t v -> p v t"), func=ACT.Copy, scale=1.0 / D)
        nc.scalar.activation(out=dev[:], in_=var_bank[:].rearrange("p t v -> p v t"), func=ACT.Sqrt, scale=0.125)
        partner = {}
        for name, values in (("w3", dev), ("w2", mean)):
            codes = sbuf(f"stat_codes_{name}", [P, V], U32)
            scales = sbuf(f"stat_scales_{name}", [P, V], U8)
            quantize(codes[:], scales[:], values[:].rearrange("p v t -> p (v t)"))
            partner[name] = (codes[:], scales[:])

        for name in ("w2", "w3"):
            rounded = sbuf(f"{name}_round", [P, PACK, P, PACK], BF16)
            source = w_raw[name][:].rearrange("p j (m t) -> p m j t", t=PACK)
            for engine, a, b in W_SHARES[name]:
                copy_on[engine](out=rounded[:].rearrange("p t m j -> p m j t")[:, a:b], in_=source[:, a:b])
            for t0 in (0, 2):
                quantize_two_tiles(name, t0, rounded[:, t0 : t0 + 2])

        y_tags = ("bank_y0", "bank_y1", "bank0", "bank1")
        y_banks = [psum.tile([P, V], F32, name=f"y{t}", tag=y_tags[t]) for t in range(PACK)]
        for name in ("w2", "w3"):
            for t in range(PACK):
                product(y_banks[t][:], operand(name, t), partner[name], name == "w2", name == "w3")
        y = sbuf("y", [P, PACK, V], F32)
        for t in range(PACK):
            copy_on["scalar" if t % 2 == 0 else "vector"](out=y[:, t, :], in_=y_banks[t][:])
        nc.sync.dma_start(out=out_0.rearrange("(p t) v -> p t v", t=PACK), in_=y[:])

        y_round = sbuf("y_round", [P, V, PACK], BF16)
        y_codes = sbuf("y_codes", [P, V], U32)
        y_scales = sbuf("y_scales", [P, V], U8)
        nc.vector.tensor_copy(
            out=y_round[:].rearrange("p (c i) t -> p c t i", i=4),
            in_=y[:].rearrange("p t (c i) -> p c t i", i=4),
        )
        quantize(y_codes[:], y_scales[:], y_round[:].rearrange("p v t -> p (v t)"))
        nc.sync.dma_start(out=out_1[0].rearrange("p c r -> p (c r)").bitcast(I32), in_=y_codes[:].bitcast(I32))
        for g in range(P // QUADRANT):
            queue = nc.scalar if g % 2 == 0 else nc.sync
            queue.dma_start(
                out=out_2[0, 4 * g : 4 * g + 4, :].bitcast(I32),
                in_=y_scales[QUADRANT * g : QUADRANT * g + 4, :].bitcast(I32),
            )
